import numpy as np
import ml_dtypes


def mxq(x, axis, fmt="e4m3"):
    dtype, down = {"e4m3": (ml_dtypes.float8_e4m3fn, 7), "e5m2": (ml_dtypes.float8_e5m2, 14)}[fmt]
    v = np.moveaxis(np.asarray(x, np.float32).astype(ml_dtypes.bfloat16).astype(np.float64), axis, -1)
    blocks = v.reshape(v.shape[:-1] + (-1, 32))
    amax = np.abs(blocks).max(-1, keepdims=True)
    byte = np.maximum(np.where(amax > 0, np.frexp(amax)[1] - 1 + 127, 0) - down, 1)
    scale = np.exp2(byte - 127.0)
    codes = (blocks / scale).astype(np.float32).astype(dtype).astype(np.float64)
    return np.moveaxis((codes * scale).reshape(v.shape), -1, axis)


WIDE = False


def mx_kscale(k):
    if not WIDE:
        return np.ones(k)
    levels = np.array([10, -10, 5, -5, 0])
    if k % 512:
        return np.exp2(np.random.permutation(np.resize(levels, k // 32))).repeat(32)
    a = np.empty((k // 512, 16))
    for p in range(k // 512):
        a[p, :8] = np.random.permutation(np.resize(levels, 8))
        for g in range(8):
            far = levels[np.abs(levels - a[p, g]) >= 10]
            a[p, g + 8] = far[np.random.randint(len(far))]
    return np.exp2(a.ravel()).repeat(32)


BF16 = ml_dtypes.bfloat16


def bf(x):
    return np.asarray(x, np.float32).astype(BF16)


def f64(x):
    return np.asarray(x).astype(np.float64)


E2M1 = np.array([0.0, 0.5, 1.0, 1.5, 2.0, 3.0, 4.0, 6.0, -0.0, -0.5, -1.0, -1.5, -2.0, -3.0, -4.0, -6.0])


def pack_weight(w, fmt):
    k, n = w.shape
    w = f64(bf(w)).reshape(k // 32, 32, n)
    amax = np.abs(w).max(1)
    if fmt == "e4m3":
        byte = np.frexp(amax)[1] - 1 + 127 - 7
    else:
        mant, ex = np.frexp(amax / 6.0)
        byte = np.where(mant > 0.5, ex, ex - 1) + 127
    byte = np.clip(np.where(amax > 0, byte, 1), 1, 254)
    scaled = (w * np.exp2(127.0 - byte)[:, None, :]).reshape(k, n).astype(np.float32)
    by_word = np.ascontiguousarray(scaled.reshape(k // 512, 128, 4, n).transpose(0, 1, 3, 2))
    if fmt == "e4m3":
        words = by_word.astype(ml_dtypes.float8_e4m3fn).view(np.uint8)
    else:
        c = by_word.astype(ml_dtypes.float4_e2m1fn).view(np.uint8) & 0xF
        words = c[..., 0::2] | (c[..., 1::2] << 4)
    return np.ascontiguousarray(words), np.ascontiguousarray(byte.astype(np.uint8).reshape(k // 512, 16, n))


def unpack_weight(words, scales, fmt):
    g, p, n, _ = words.shape
    if fmt == "e4m3":
        vals = np.ascontiguousarray(words).view(ml_dtypes.float8_e4m3fn).astype(np.float64)
    else:
        nib = np.empty((g, p, n, 4), np.uint8)
        nib[..., 0::2] = words & 0xF
        nib[..., 1::2] = words >> 4
        vals = E2M1[nib]
    vals = vals * np.repeat(np.exp2(scales.astype(np.float64) - 127.0), 8, axis=1)[..., None]
    return vals.transpose(0, 1, 3, 2).reshape(g * 512, n)
def pack4(w):
    words, scales = pack_weight(w, "e2m1")
    return words.reshape(words.shape[0], 128, -1), scales


def unpack4(words, scales):
    return unpack_weight(words.reshape(words.shape[0], 128, -1, 2), scales, "e2m1")


E4M3FN = np.array([(-1.0 if i & 128 else 1.0) * ((1.0 + (i & 7) / 8.0) * 2.0 ** (((i >> 3) & 15) - 7) if i & 120 else (i & 7) * 2.0 ** -9) for i in range(256)])


def e4m3fn_bytes(y):
    return np.clip(np.asarray(y, np.float64), -448.0, 448.0).astype(np.float32).astype(ml_dtypes.float8_e4m3fn).view(np.uint8)


def e4m3fn_values(b):
    return E4M3FN[b]


T, K, N, B = 1024, 2048, 1024, 128


def setup_inputs():
    s, r = mx_kscale(K), mx_kscale(K)
    xk = np.random.standard_normal((T, K)) * s
    xr = np.random.standard_normal((T, K)) * r
    xk_scale = (np.abs(xk).reshape(T, K // B, B).max(axis=2) / 448.0).astype(np.float32)
    xr_scale = (np.abs(xr).reshape(T, K // B, B).max(axis=2) / 448.0).astype(np.float32)
    wk_words, wk_scales = pack4(np.random.standard_normal((K, N)) / np.sqrt(K) / s[:, None])
    return {"xk_bytes": e4m3fn_bytes(xk / np.repeat(f64(xk_scale), B, axis=1)),
            "xk_scale": xk_scale,
            "xr_bytes": e4m3fn_bytes(xr / np.repeat(f64(xr_scale), B, axis=1)),
            "xr_scale": xr_scale,
            "wk_words": wk_words,
            "wk_scales": wk_scales,
            "wr": bf(np.random.standard_normal((K, N)) / np.sqrt(K) / r[:, None])}


def reference(xk_bytes, xk_scale, xr_bytes, xr_scale, wk_words, wk_scales, wr):
    xk = e4m3fn_values(xk_bytes) * np.repeat(f64(xk_scale), B, axis=1)
    xr = e4m3fn_values(xr_bytes) * np.repeat(f64(xr_scale), B, axis=1)
    key = mxq(xk, 1, "e4m3") @ unpack4(wk_words, wk_scales)
    rec = mxq(xr, 1, "e4m3") @ mxq(f64(wr), 0, "e4m3")
    hidden = np.square(np.maximum(key, 0.0))
    gate = 1.0 / (1.0 + np.exp(-rec))
    return gate * hidden

@@ -1,0 +1,218 @@
+from contextlib import ExitStack
+
+import concourse.mybir as mybir
+from concourse.masks import make_identity
+
+T, K, N = 1024, 2048, 1024
+FLOPS = 2 * 2 * T * K * N
+
+F32 = mybir.dt.float32
+BF16 = mybir.dt.bfloat16
+I32 = mybir.dt.int32
+U32 = mybir.dt.uint32
+U8 = mybir.dt.uint8
+FP8 = mybir.dt.float8_e4m3fn
+FP8X4 = mybir.dt.float8_e4m3fn_x4
+FP4X4 = mybir.dt.float4_e2m1fn_x4
+ACT = mybir.ActivationFunctionType
+ALU = mybir.AluOpType
+
+P = 128
+TILES = T // P
+PASSES = K // 512
+BLOCK = 128
+HALF = 512
+
+KEY_LEAD = 6
+SCALAR_PASSES = 1
+
+
+def tile_rwkv_channel_mix_gate_d1_kernel(tc, xk_bytes, xk_scale, xr_bytes, xr_scale, wk_words, wk_scales, wr, out):
+    nc = tc.nc
+    bytes_in = {"k": xk_bytes.rearrange("(p c) k -> p c k", c=TILES), "r": xr_bytes.rearrange("(p c) k -> p c k", c=TILES)}
+    scale_in = {"k": xk_scale.rearrange("(p c) j -> p (c j)", c=TILES), "r": xr_scale.rearrange("(p c) j -> p (c j)", c=TILES)}
+    wr_in = wr.rearrange("(g p j) n -> g p j n", p=P, j=4)
+    out_rows = out.rearrange("(p c) n -> p c n", c=TILES)
+
+    units = [("k", c) for c in range(KEY_LEAD)]
+    for c in range(TILES):
+        units.append(("r", c))
+        if c + KEY_LEAD < TILES:
+            units.append(("k", c + KEY_LEAD))
+
+    with ExitStack() as ctx:
+        keep = ctx.enter_context(tc.tile_pool(name="keep", bufs=1))
+        wide_pool = ctx.enter_context(tc.tile_pool(name="wide", bufs=3))
+        work = ctx.enter_context(tc.tile_pool(name="work", bufs=3))
+        turn_psum = ctx.enter_context(tc.psum_pool(name="turn", bufs=4))
+        acc_psum = ctx.enter_context(tc.psum_pool(name="acc", bufs=4))
+
+        ident = keep.tile([P, P], F32, name="ident")
+        make_identity(nc, ident[:])
+        wk_s = keep.tile([P, PASSES, N], U8, name="wk_s", align_bytes=64)
+        nc.gpsimd.memset(wk_s[:].bitcast(I32), 0)
+        dummy = keep.tile([P, 1], F32, name="dummy")
+        nc.scalar.activation(dummy[:], ident[:, 0:1], ACT.Sigmoid)
+
+        x_scale = {}
+        x_bytes = {}
+        wk_w = []
+        wr_raw = {}
+
+        def load_scale(op):
+            x_scale[op] = keep.tile([P, TILES * K // BLOCK], F32, name="x_scale_%s" % op)
+            nc.sync.dma_start(out=x_scale[op][:], in_=scale_in[op])
+
+        def load_x(op, c):
+            x_bytes[op, c] = keep.tile([P, K], U8, name="x_bytes_%s%d" % (op, c), align_bytes=64)
+            nc.sync.dma_start(out=x_bytes[op, c][:], in_=bytes_in[op][:, c, :])
+
+        def load_wk():
+            for g in range(PASSES):
+                w = keep.tile([P, 2 * N], U8, name="wk_w%d" % g, align_bytes=64)
+                nc.sync.dma_start(out=w[:].bitcast(I32), in_=wk_words[g].bitcast(I32))
+                wk_w.append(w)
+            for q in range(4):
+                nc.sync.dma_start(
+                    out=wk_s[32 * q : 32 * q + 4, :, :].bitcast(I32),
+                    in_=wk_scales[:, 4 * q : 4 * q + 4, :].rearrange("g s n -> s g n").bitcast(I32),
+                )
+
+        def load_wr(g, h):
+            wr_raw[g, h] = keep.tile([P, 4, HALF], BF16, name="wr_raw%d%d" % (g, h), align_bytes=64)
+            nc.sync.dma_start(out=wr_raw[g, h][:], in_=wr_in[g][:, :, h * HALF : (h + 1) * HALF])
+
+        chunks = [(g, 0) for g in range(PASSES)] + [(g, 1) for g in range(PASSES)]
+        load_scale("k")
+        load_x(*units[0])
+        load_wk()
+        for u in units[1:3]:
+            load_x(*u)
+        load_scale("r")
+        later = list(chunks)
+        for u in units[3:]:
+            load_x(*u)
+            if later:
+                load_wr(*later.pop(0))
+
+        wide = {}
+        grouped = {}
+        codes = {}
+        scales = {}
+        wr_grouped = {}
+        wr_codes = {}
+        wr_scales = {}
+        hidden = {}
+
+        def widen(op, c):
+            w = wide_pool.tile([P, K], BF16, name="wide", align_bytes=64)
+            wide[op, c] = w
+            for g in range(PASSES):
+                on_scalar = g >= PASSES - SCALAR_PASSES
+                turned = w[:, 512 * g : 512 * (g + 1)].rearrange("p (u q i e) -> p q i u e", u=2, q=4, i=32, e=2)
+                for q in range(4):
+                    j = 4 * g + q
+                    src = x_bytes[op, c][:, BLOCK * j : BLOCK * (j + 1)].bitcast(FP8)
+                    s = x_scale[op][:, c * 16 + j : c * 16 + j + 1]
+                    if on_scalar:
+                        nc.scalar.activation(w[:, BLOCK * j : BLOCK * (j + 1)], src, ACT.Copy, scale=s)
+                    else:
+                        nc.vector.tensor_scalar(
+                            out=turned[:, q], in0=src.rearrange("p (i u e) -> p i u e", u=2, e=2), scalar1=s, scalar2=None, op0=ALU.mult
+                        )
+
+        def turn(op, c):
+            words = wide[op, c][:].bitcast(F32)
+            gr = work.tile([P, 4 * PASSES * P], BF16, name="grouped", align_bytes=64)
+            grouped[op, c] = gr
+            for b in range(PASSES // 2):
+                bank = turn_psum.tile([P, 2, 2, P], F32, name="bank")
+                for i in range(2):
+                    g = 2 * b + i
+                    for u in range(2):
+                        if g >= PASSES - SCALAR_PASSES:
+                            src = words[:, 256 * g + u : 256 * (g + 1) : 2]
+                        else:
+                            src = words[:, 256 * g + 128 * u : 256 * g + 128 * (u + 1)]
+                        nc.tensor.transpose(bank[:, i, u, :], src, ident[:])
+                nc.scalar.copy(
+                    gr[:].bitcast(F32)[:, 512 * b : 512 * (b + 1)].rearrange("p (g r u) -> p g r u", g=2, u=2),
+                    bank[:].rearrange("p g u r -> p g r u"),
+                )
+
+        def quantise(op, c):
+            codes[op, c] = keep.tile([P, PASSES * P], U32, name="codes_%s%d" % (op, c), align_bytes=64)
+            scales[op, c] = keep.tile([P, PASSES * P], U8, name="scales_%s%d" % (op, c), align_bytes=64)
+            nc.vector.quantize_mx(out=codes[op, c][:].bitcast(FP8X4), scales=scales[op, c][:], in_=grouped[op, c][:])
+
+        def prepare_wr(g, h):
+            gr = work.tile([P, 4 * HALF], BF16, name="wr_grouped", align_bytes=64)
+            nc.vector.tensor_copy(
+                out=gr[:].rearrange("p (c i t) -> p c t i", i=4, t=4),
+                in_=wr_raw[g, h][:].rearrange("p t (c i) -> p c t i", i=4),
+            )
+            wr_grouped[g, h] = gr
+
+        def quantise_wr(g, h):
+            wr_codes[g, h] = keep.tile([P, HALF], U32, name="wr_codes%d%d" % (g, h), align_bytes=64)
+            wr_scales[g, h] = keep.tile([P, HALF], U8, name="wr_scales%d%d" % (g, h), align_bytes=64)
+            nc.vector.quantize_mx(out=wr_codes[g, h][:].bitcast(FP8X4), scales=wr_scales[g, h][:], in_=wr_grouped[g, h][:])
+
+        def product(op, c, h):
+            acc = acc_psum.tile([P, HALF], F32, name="acc")
+            for g in range(PASSES):
+                if op == "k":
+                    rhs = wk_w[g][:, 2 * HALF * h : 2 * HALF * (h + 1)].bitcast(FP4X4)
+                    rhs_scale = wk_s[:, g, HALF * h : HALF * (h + 1)]
+                else:
+                    rhs = wr_codes[g, h][:].bitcast(FP8X4)
+                    rhs_scale = wr_scales[g, h][:]
+                nc.tensor.matmul_mx(
+                    acc[:],
+                    lhsT=codes[op, c][:, P * g : P * (g + 1)].bitcast(FP8X4),
+                    lhsT_scale=scales[op, c][:, P * g : P * (g + 1)],
+                    rhs=rhs,
+                    rhs_scale=rhs_scale,
+                    start=(g == 0),
+                    stop=(g == PASSES - 1),
+                )
+            return acc
+
+        def finish_key(c, h):
+            acc = product("k", c, h)
+            r = work.tile([P, HALF], F32, name="relu")
+            nc.scalar.activation(r[:], acc[:], ACT.Relu)
+            hidden[c, h] = keep.tile([P, HALF], F32, name="hidden%d%d" % (c, h))
+            nc.scalar.activation(hidden[c, h][:], r[:], ACT.Square)
+
+        def finish_rec(c, h):
+            acc = product("r", c, h)
+            g = work.tile([P, HALF], F32, name="gate")
+            nc.scalar.activation(g[:], acc[:], ACT.Sigmoid)
+            o = work.tile([P, HALF], F32, name="result")
+            nc.vector.tensor_tensor(out=o[:], in0=g[:], in1=hidden[c, h][:], op=ALU.mult)
+            nc.sync.dma_start(out=out_rows[:, c, h * HALF : (h + 1) * HALF], in_=o[:])
+
+        pending = list(chunks)
+        waiting = []
+        n = len(units)
+        for s in range(n + 2):
+            if s < n:
+                widen(*units[s])
+            if 0 <= s - 1 < n:
+                turn(*units[s - 1])
+                quantise(*units[s - 1])
+            if 3 <= s and pending:
+                prepare_wr(*pending[0])
+                quantise_wr(*pending.pop(0))
+            if 0 <= s - 2 < n:
+                op, c = units[s - 2]
+                for h in range(2):
+                    if op == "k":
+                        finish_key(c, h)
+                    else:
+                        waiting.append((c, h))
+            ready = [w for w in waiting if (PASSES - 1, w[1]) in wr_codes]
+            for c, h in ready:
+                finish_rec(c, h)
+                waiting.remove((c, h))

@@ -21,10 +21,23 @@ P = 128
 TILES = T // P
 PASSES = K // 512
 BLOCK = 128
+BLOCKS = K // BLOCK
 HALF = 512
 
-KEY_LEAD = 6
-SCALAR_PASSES = 1
+UNITS = [("k", c) for c in range(TILES)] + [("r", c) for c in range(TILES)]
+CHUNKS = [(g, h) for h in range(2) for g in range(PASSES)]
+FIRST_CHUNK_STEP = 2
+SQUARE_STEP = 8
+
+
+def pieces(i):
+    if i == len(UNITS) - 1:
+        return [(0, HALF), (HALF, HALF // 2), (HALF + HALF // 2, HALF // 2)]
+    return [(0, HALF), (HALF, HALF)]
+
+
+def scalar_passes(i):
+    return 2 if i == 0 else (1 if i < 10 else 0)
 
 
 def tile_rwkv_channel_mix_gate_d1_kernel(tc, xk_bytes, xk_scale, xr_bytes, xr_scale, wk_words, wk_scales, wr, out):
@@ -34,25 +47,12 @@ def tile_rwkv_channel_mix_gate_d1_kernel(tc, xk_bytes, xk_scale, xr_bytes, xr_sc
     wr_in = wr.rearrange("(g p j) n -> g p j n", p=P, j=4)
     out_rows = out.rearrange("(p c) n -> p c n", c=TILES)
 
-    units = [("k", c) for c in range(KEY_LEAD)]
-    for c in range(TILES):
-        units.append(("r", c))
-        if c + KEY_LEAD < TILES:
-            units.append(("k", c + KEY_LEAD))
-
     with ExitStack() as ctx:
         keep = ctx.enter_context(tc.tile_pool(name="keep", bufs=1))
-        wide_pool = ctx.enter_context(tc.tile_pool(name="wide", bufs=3))
-        work = ctx.enter_context(tc.tile_pool(name="work", bufs=3))
+        work = ctx.enter_context(tc.tile_pool(name="work", bufs=4))
         turn_psum = ctx.enter_context(tc.psum_pool(name="turn", bufs=4))
         acc_psum = ctx.enter_context(tc.psum_pool(name="acc", bufs=4))
-
-        ident = keep.tile([P, P], F32, name="ident")
-        make_identity(nc, ident[:])
-        wk_s = keep.tile([P, PASSES, N], U8, name="wk_s", align_bytes=64)
-        nc.gpsimd.memset(wk_s[:].bitcast(I32), 0)
-        dummy = keep.tile([P, 1], F32, name="dummy")
-        nc.scalar.activation(dummy[:], ident[:, 0:1], ACT.Sigmoid)
+        ctx.enter_context(tc.manual_schedule())
 
         x_scale = {}
         x_bytes = {}
@@ -60,42 +60,45 @@ def tile_rwkv_channel_mix_gate_d1_kernel(tc, xk_bytes, xk_scale, xr_bytes, xr_sc
         wr_raw = {}
 
         def load_scale(op):
-            x_scale[op] = keep.tile([P, TILES * K // BLOCK], F32, name="x_scale_%s" % op)
-            nc.sync.dma_start(out=x_scale[op][:], in_=scale_in[op])
+            x_scale[op] = keep.tile([P, TILES * BLOCKS], F32, name="x_scale_%s" % op)
+            nc.scalar.dma_start(out=x_scale[op][:], in_=scale_in[op])
 
         def load_x(op, c):
             x_bytes[op, c] = keep.tile([P, K], U8, name="x_bytes_%s%d" % (op, c), align_bytes=64)
             nc.sync.dma_start(out=x_bytes[op, c][:], in_=bytes_in[op][:, c, :])
 
-        def load_wk():
-            for g in range(PASSES):
-                w = keep.tile([P, 2 * N], U8, name="wk_w%d" % g, align_bytes=64)
-                nc.sync.dma_start(out=w[:].bitcast(I32), in_=wk_words[g].bitcast(I32))
-                wk_w.append(w)
-            for q in range(4):
-                nc.sync.dma_start(
-                    out=wk_s[32 * q : 32 * q + 4, :, :].bitcast(I32),
-                    in_=wk_scales[:, 4 * q : 4 * q + 4, :].rearrange("g s n -> s g n").bitcast(I32),
-                )
-
         def load_wr(g, h):
             wr_raw[g, h] = keep.tile([P, 4, HALF], BF16, name="wr_raw%d%d" % (g, h), align_bytes=64)
             nc.sync.dma_start(out=wr_raw[g, h][:], in_=wr_in[g][:, :, h * HALF : (h + 1) * HALF])
 
-        chunks = [(g, 0) for g in range(PASSES)] + [(g, 1) for g in range(PASSES)]
         load_scale("k")
-        load_x(*units[0])
-        load_wk()
-        for u in units[1:3]:
-            load_x(*u)
         load_scale("r")
-        later = list(chunks)
-        for u in units[3:]:
-            load_x(*u)
-            if later:
-                load_wr(*later.pop(0))
+        ident = keep.tile([P, P], F32, name="ident")
+        make_identity(nc, ident[:])
+        wk_s = keep.tile([P, PASSES, N], U8, name="wk_s", align_bytes=64)
+        nc.gpsimd.memset(wk_s[:].bitcast(I32), 0)
+        dummy = keep.tile([P, 1], F32, name="dummy")
+        nc.scalar.activation(dummy[:], ident[:, 0:1], ACT.Sigmoid)
+
+        load_x(*UNITS[0])
+        load_x(*UNITS[1])
+        for g in range(PASSES):
+            w = keep.tile([P, 2 * N], U8, name="wk_w%d" % g, align_bytes=64)
+            nc.sync.dma_start(out=w[:].bitcast(I32), in_=wk_words[g].bitcast(I32))
+            wk_w.append(w)
+        for q in range(4):
+            nc.sync.dma_start(
+                out=wk_s[32 * q : 32 * q + 4, :, :].bitcast(I32),
+                in_=wk_scales[:, 4 * q : 4 * q + 4, :].rearrange("g s n -> s g n").bitcast(I32),
+            )
+        load_x(*UNITS[2])
+        for i in range(3, len(UNITS)):
+            if i - 3 < len(CHUNKS):
+                load_wr(*CHUNKS[i - 3])
+            load_x(*UNITS[i])
 
         wide = {}
+        banks = {}
         grouped = {}
         codes = {}
         scales = {}
@@ -103,49 +106,56 @@ def tile_rwkv_channel_mix_gate_d1_kernel(tc, xk_bytes, xk_scale, xr_bytes, xr_sc
         wr_codes = {}
         wr_scales = {}
         hidden = {}
+        accs = {}
+        gates = {}
 
-        def widen(op, c):
-            w = wide_pool.tile([P, K], BF16, name="wide", align_bytes=64)
-            wide[op, c] = w
-            for g in range(PASSES):
-                on_scalar = g >= PASSES - SCALAR_PASSES
-                turned = w[:, 512 * g : 512 * (g + 1)].rearrange("p (u q i e) -> p q i u e", u=2, q=4, i=32, e=2)
+        def start_wide(i):
+            wide[i] = work.tile([P, K], BF16, name="wide", align_bytes=64)
+
+        def block_operands(i, j):
+            op, c = UNITS[i]
+            return x_bytes[op, c][:, BLOCK * j : BLOCK * (j + 1)].bitcast(FP8), x_scale[op][:, c * BLOCKS + j : c * BLOCKS + j + 1]
+
+        def widen_on_vector(i):
+            for g in range(PASSES - scalar_passes(i)):
+                turned = wide[i][:, 512 * g : 512 * (g + 1)].rearrange("p (u q i e) -> p q i u e", u=2, q=4, i=32, e=2)
                 for q in range(4):
-                    j = 4 * g + q
-                    src = x_bytes[op, c][:, BLOCK * j : BLOCK * (j + 1)].bitcast(FP8)
-                    s = x_scale[op][:, c * 16 + j : c * 16 + j + 1]
-                    if on_scalar:
-                        nc.scalar.activation(w[:, BLOCK * j : BLOCK * (j + 1)], src, ACT.Copy, scale=s)
-                    else:
-                        nc.vector.tensor_scalar(
-                            out=turned[:, q], in0=src.rearrange("p (i u e) -> p i u e", u=2, e=2), scalar1=s, scalar2=None, op0=ALU.mult
-                        )
+                    src, s = block_operands(i, 4 * g + q)
+                    nc.vector.tensor_scalar(out=turned[:, q], in0=src.rearrange("p (i u e) -> p i u e", u=2, e=2), scalar1=s, scalar2=None, op0=ALU.mult)
 
-        def turn(op, c):
-            words = wide[op, c][:].bitcast(F32)
-            gr = work.tile([P, 4 * PASSES * P], BF16, name="grouped", align_bytes=64)
-            grouped[op, c] = gr
+        def widen_on_scalar(i):
+            for j in range(4 * (PASSES - scalar_passes(i)), BLOCKS):
+                src, s = block_operands(i, j)
+                nc.scalar.activation(wide[i][:, BLOCK * j : BLOCK * (j + 1)], src, ACT.Copy, scale=s)
+
+        def turn(i):
+            words = wide[i][:].bitcast(F32)
             for b in range(PASSES // 2):
                 bank = turn_psum.tile([P, 2, 2, P], F32, name="bank")
-                for i in range(2):
-                    g = 2 * b + i
+                banks[i, b] = bank
+                for k in range(2):
+                    g = 2 * b + k
                     for u in range(2):
-                        if g >= PASSES - SCALAR_PASSES:
+                        if g >= PASSES - scalar_passes(i):
                             src = words[:, 256 * g + u : 256 * (g + 1) : 2]
                         else:
                             src = words[:, 256 * g + 128 * u : 256 * g + 128 * (u + 1)]
-                        nc.tensor.transpose(bank[:, i, u, :], src, ident[:])
+                        nc.tensor.transpose(bank[:, k, u, :], src, ident[:])
+
+        def collect(i):
+            grouped[i] = work.tile([P, 4 * PASSES * P], BF16, name="grouped", align_bytes=64)
+            for b in range(PASSES // 2):
                 nc.scalar.copy(
-                    gr[:].bitcast(F32)[:, 512 * b : 512 * (b + 1)].rearrange("p (g r u) -> p g r u", g=2, u=2),
-                    bank[:].rearrange("p g u r -> p g r u"),
+                    grouped[i][:].bitcast(F32)[:, 512 * b : 512 * (b + 1)].rearrange("p (g r u) -> p g r u", g=2, u=2),
+                    banks[i, b][:].rearrange("p g u r -> p g r u"),
                 )
 
-        def quantise(op, c):
-            codes[op, c] = keep.tile([P, PASSES * P], U32, name="codes_%s%d" % (op, c), align_bytes=64)
-            scales[op, c] = keep.tile([P, PASSES * P], U8, name="scales_%s%d" % (op, c), align_bytes=64)
-            nc.vector.quantize_mx(out=codes[op, c][:].bitcast(FP8X4), scales=scales[op, c][:], in_=grouped[op, c][:])
+        def quantise(i):
+            codes[i] = work.tile([P, PASSES * P], U32, name="codes", align_bytes=64)
+            scales[i] = work.tile([P, PASSES * P], U8, name="scales", align_bytes=64)
+            nc.vector.quantize_mx(out=codes[i][:].bitcast(FP8X4), scales=scales[i][:], in_=grouped[i][:])
 
-        def prepare_wr(g, h):
+        def interleave_wr(g, h):
             gr = work.tile([P, 4 * HALF], BF16, name="wr_grouped", align_bytes=64)
             nc.vector.tensor_copy(
                 out=gr[:].rearrange("p (c i t) -> p c t i", i=4, t=4),
@@ -158,61 +168,70 @@ def tile_rwkv_channel_mix_gate_d1_kernel(tc, xk_bytes, xk_scale, xr_bytes, xr_sc
             wr_scales[g, h] = keep.tile([P, HALF], U8, name="wr_scales%d%d" % (g, h), align_bytes=64)
             nc.vector.quantize_mx(out=wr_codes[g, h][:].bitcast(FP8X4), scales=wr_scales[g, h][:], in_=wr_grouped[g, h][:])
 
-        def product(op, c, h):
+        def multiply(i, n0, width):
+            op = UNITS[i][0]
+            h, m0 = n0 // HALF, n0 % HALF
             acc = acc_psum.tile([P, HALF], F32, name="acc")
+            accs[i, n0] = acc
             for g in range(PASSES):
                 if op == "k":
-                    rhs = wk_w[g][:, 2 * HALF * h : 2 * HALF * (h + 1)].bitcast(FP4X4)
-                    rhs_scale = wk_s[:, g, HALF * h : HALF * (h + 1)]
+                    rhs = wk_w[g][:, 2 * n0 : 2 * (n0 + width)].bitcast(FP4X4)
+                    rhs_scale = wk_s[:, g, n0 : n0 + width]
                 else:
-                    rhs = wr_codes[g, h][:].bitcast(FP8X4)
-                    rhs_scale = wr_scales[g, h][:]
+                    rhs = wr_codes[g, h][:, m0 : m0 + width].bitcast(FP8X4)
+                    rhs_scale = wr_scales[g, h][:, m0 : m0 + width]
                 nc.tensor.matmul_mx(
-                    acc[:],
-                    lhsT=codes[op, c][:, P * g : P * (g + 1)].bitcast(FP8X4),
-                    lhsT_scale=scales[op, c][:, P * g : P * (g + 1)],
+                    acc[:, 0:width],
+                    lhsT=codes[i][:, P * g : P * (g + 1)].bitcast(FP8X4),
+                    lhsT_scale=scales[i][:, P * g : P * (g + 1)],
                     rhs=rhs,
                     rhs_scale=rhs_scale,
                     start=(g == 0),
                     stop=(g == PASSES - 1),
                 )
-            return acc
 
-        def finish_key(c, h):
-            acc = product("k", c, h)
-            r = work.tile([P, HALF], F32, name="relu")
-            nc.scalar.activation(r[:], acc[:], ACT.Relu)
-            hidden[c, h] = keep.tile([P, HALF], F32, name="hidden%d%d" % (c, h))
-            nc.scalar.activation(hidden[c, h][:], r[:], ACT.Square)
+        def empty(i, n0, width):
+            op, c = UNITS[i]
+            if op == "k":
+                if n0 == 0:
+                    hidden[c] = keep.tile([P, N], F32, name="hidden%d" % c)
+                nc.scalar.activation(hidden[c][:, n0 : n0 + width], accs[i, n0][:, 0:width], ACT.Relu)
+            else:
+                gates[c, n0] = work.tile([P, HALF], F32, name="gate")
+                nc.scalar.activation(gates[c, n0][:, 0:width], accs[i, n0][:, 0:width], ACT.Sigmoid)
 
-        def finish_rec(c, h):
-            acc = product("r", c, h)
-            g = work.tile([P, HALF], F32, name="gate")
-            nc.scalar.activation(g[:], acc[:], ACT.Sigmoid)
-            o = work.tile([P, HALF], F32, name="result")
-            nc.vector.tensor_tensor(out=o[:], in0=g[:], in1=hidden[c, h][:], op=ALU.mult)
-            nc.sync.dma_start(out=out_rows[:, c, h * HALF : (h + 1) * HALF], in_=o[:])
+        def square(c):
+            nc.scalar.activation(hidden[c][:], hidden[c][:], ACT.Square)
 
-        pending = list(chunks)
-        waiting = []
-        n = len(units)
+        def finish(c, n0, width):
+            cols = slice(n0, n0 + width)
+            result = work.tile([P, HALF], F32, name="result")
+            nc.vector.tensor_tensor(out=result[:, 0:width], in0=gates[c, n0][:, 0:width], in1=hidden[c][:, cols], op=ALU.mult)
+            nc.sync.dma_start(out=out_rows[:, c, cols], in_=result[:, 0:width])
+
+        n = len(UNITS)
         for s in range(n + 2):
             if s < n:
-                widen(*units[s])
-            if 0 <= s - 1 < n:
-                turn(*units[s - 1])
-                quantise(*units[s - 1])
-            if 3 <= s and pending:
-                prepare_wr(*pending[0])
-                quantise_wr(*pending.pop(0))
-            if 0 <= s - 2 < n:
-                op, c = units[s - 2]
-                for h in range(2):
-                    if op == "k":
-                        finish_key(c, h)
-                    else:
-                        waiting.append((c, h))
-            ready = [w for w in waiting if (PASSES - 1, w[1]) in wr_codes]
-            for c, h in ready:
-                finish_rec(c, h)
-                waiting.remove((c, h))
+                start_wide(s)
+                widen_on_vector(s)
+            if 1 <= s <= n:
+                turn(s - 1)
+                collect(s - 1)
+            if 0 <= s - SQUARE_STEP < TILES:
+                square(s - SQUARE_STEP)
+            if s < n:
+                widen_on_scalar(s)
+            chunk = s - FIRST_CHUNK_STEP
+            if 0 <= chunk < len(CHUNKS):
+                interleave_wr(*CHUNKS[chunk])
+            if 1 <= s <= n:
+                quantise(s - 1)
+            if s >= 2:
+                for n0, width in pieces(s - 2):
+                    multiply(s - 2, n0, width)
+                    empty(s - 2, n0, width)
+                if UNITS[s - 2][0] == "r":
+                    for n0, width in pieces(s - 2):
+                        finish(UNITS[s - 2][1], n0, width)
+            if 0 <= chunk < len(CHUNKS):
+                quantise_wr(*CHUNKS[chunk])

from contextlib import ExitStack

import concourse.mybir as mybir
from concourse.masks import make_identity

T, K, N = 1024, 2048, 1024
FLOPS = 2 * 2 * T * K * N

F32 = mybir.dt.float32
BF16 = mybir.dt.bfloat16
I32 = mybir.dt.int32
U32 = mybir.dt.uint32
U8 = mybir.dt.uint8
FP8 = mybir.dt.float8_e4m3fn
FP8X4 = mybir.dt.float8_e4m3fn_x4
FP4X4 = mybir.dt.float4_e2m1fn_x4
ACT = mybir.ActivationFunctionType
ALU = mybir.AluOpType

P = 128
TILES = T // P
PASSES = K // 512
BLOCK = 128
BLOCKS = K // BLOCK
HALF = 512

UNITS = [("k", c) for c in range(TILES)] + [("r", c) for c in range(TILES)]
CHUNKS = [(g, h) for h in range(2) for g in range(PASSES)]
FIRST_CHUNK_STEP = 2
SQUARE_STEP = 8


def pieces(i):
    if i == len(UNITS) - 1:
        return [(0, HALF), (HALF, HALF // 2), (HALF + HALF // 2, HALF // 2)]
    return [(0, HALF), (HALF, HALF)]


def scalar_passes(i):
    return 2 if i == 0 else (1 if i < 10 else 0)


def tile_rwkv_channel_mix_gate_d1_kernel(tc, xk_bytes, xk_scale, xr_bytes, xr_scale, wk_words, wk_scales, wr, out):
    nc = tc.nc
    bytes_in = {"k": xk_bytes.rearrange("(p c) k -> p c k", c=TILES), "r": xr_bytes.rearrange("(p c) k -> p c k", c=TILES)}
    scale_in = {"k": xk_scale.rearrange("(p c) j -> p (c j)", c=TILES), "r": xr_scale.rearrange("(p c) j -> p (c j)", c=TILES)}
    wr_in = wr.rearrange("(g p j) n -> g p j n", p=P, j=4)
    out_rows = out.rearrange("(p c) n -> p c n", c=TILES)

    with ExitStack() as ctx:
        keep = ctx.enter_context(tc.tile_pool(name="keep", bufs=1))
        work = ctx.enter_context(tc.tile_pool(name="work", bufs=4))
        turn_psum = ctx.enter_context(tc.psum_pool(name="turn", bufs=4))
        acc_psum = ctx.enter_context(tc.psum_pool(name="acc", bufs=4))
        ctx.enter_context(tc.manual_schedule())

        x_scale = {}
        x_bytes = {}
        wk_w = []
        wr_raw = {}

        def load_scale(op):
            x_scale[op] = keep.tile([P, TILES * BLOCKS], F32, name="x_scale_%s" % op)
            nc.scalar.dma_start(out=x_scale[op][:], in_=scale_in[op])

        def load_x(op, c):
            x_bytes[op, c] = keep.tile([P, K], U8, name="x_bytes_%s%d" % (op, c), align_bytes=64)
            nc.sync.dma_start(out=x_bytes[op, c][:], in_=bytes_in[op][:, c, :])

        def load_wr(g, h):
            wr_raw[g, h] = keep.tile([P, 4, HALF], BF16, name="wr_raw%d%d" % (g, h), align_bytes=64)
            nc.sync.dma_start(out=wr_raw[g, h][:], in_=wr_in[g][:, :, h * HALF : (h + 1) * HALF])

        load_scale("k")
        load_scale("r")
        ident = keep.tile([P, P], F32, name="ident")
        make_identity(nc, ident[:])
        wk_s = keep.tile([P, PASSES, N], U8, name="wk_s", align_bytes=64)
        nc.gpsimd.memset(wk_s[:].bitcast(I32), 0)
        dummy = keep.tile([P, 1], F32, name="dummy")
        nc.scalar.activation(dummy[:], ident[:, 0:1], ACT.Sigmoid)

        load_x(*UNITS[0])
        load_x(*UNITS[1])
        for g in range(PASSES):
            w = keep.tile([P, 2 * N], U8, name="wk_w%d" % g, align_bytes=64)
            nc.sync.dma_start(out=w[:].bitcast(I32), in_=wk_words[g].bitcast(I32))
            wk_w.append(w)
        for q in range(4):
            nc.sync.dma_start(
                out=wk_s[32 * q : 32 * q + 4, :, :].bitcast(I32),
                in_=wk_scales[:, 4 * q : 4 * q + 4, :].rearrange("g s n -> s g n").bitcast(I32),
            )
        load_x(*UNITS[2])
        for i in range(3, len(UNITS)):
            if i - 3 < len(CHUNKS):
                load_wr(*CHUNKS[i - 3])
            load_x(*UNITS[i])

        wide = {}
        banks = {}
        grouped = {}
        codes = {}
        scales = {}
        wr_grouped = {}
        wr_codes = {}
        wr_scales = {}
        hidden = {}
        accs = {}
        gates = {}

        def start_wide(i):
            wide[i] = work.tile([P, K], BF16, name="wide", align_bytes=64)

        def block_operands(i, j):
            op, c = UNITS[i]
            return x_bytes[op, c][:, BLOCK * j : BLOCK * (j + 1)].bitcast(FP8), x_scale[op][:, c * BLOCKS + j : c * BLOCKS + j + 1]

        def widen_on_vector(i):
            for g in range(PASSES - scalar_passes(i)):
                turned = wide[i][:, 512 * g : 512 * (g + 1)].rearrange("p (u q i e) -> p q i u e", u=2, q=4, i=32, e=2)
                for q in range(4):
                    src, s = block_operands(i, 4 * g + q)
                    nc.vector.tensor_scalar(out=turned[:, q], in0=src.rearrange("p (i u e) -> p i u e", u=2, e=2), scalar1=s, scalar2=None, op0=ALU.mult)

        def widen_on_scalar(i):
            for j in range(4 * (PASSES - scalar_passes(i)), BLOCKS):
                src, s = block_operands(i, j)
                nc.scalar.activation(wide[i][:, BLOCK * j : BLOCK * (j + 1)], src, ACT.Copy, scale=s)

        def turn(i):
            words = wide[i][:].bitcast(F32)
            for b in range(PASSES // 2):
                bank = turn_psum.tile([P, 2, 2, P], F32, name="bank")
                banks[i, b] = bank
                for k in range(2):
                    g = 2 * b + k
                    for u in range(2):
                        if g >= PASSES - scalar_passes(i):
                            src = words[:, 256 * g + u : 256 * (g + 1) : 2]
                        else:
                            src = words[:, 256 * g + 128 * u : 256 * g + 128 * (u + 1)]
                        nc.tensor.transpose(bank[:, k, u, :], src, ident[:])

        def collect(i):
            grouped[i] = work.tile([P, 4 * PASSES * P], BF16, name="grouped", align_bytes=64)
            for b in range(PASSES // 2):
                nc.scalar.copy(
                    grouped[i][:].bitcast(F32)[:, 512 * b : 512 * (b + 1)].rearrange("p (g r u) -> p g r u", g=2, u=2),
                    banks[i, b][:].rearrange("p g u r -> p g r u"),
                )

        def quantise(i):
            codes[i] = work.tile([P, PASSES * P], U32, name="codes", align_bytes=64)
            scales[i] = work.tile([P, PASSES * P], U8, name="scales", align_bytes=64)
            nc.vector.quantize_mx(out=codes[i][:].bitcast(FP8X4), scales=scales[i][:], in_=grouped[i][:])

        def interleave_wr(g, h):
            gr = work.tile([P, 4 * HALF], BF16, name="wr_grouped", align_bytes=64)
            nc.vector.tensor_copy(
                out=gr[:].rearrange("p (c i t) -> p c t i", i=4, t=4),
                in_=wr_raw[g, h][:].rearrange("p t (c i) -> p c t i", i=4),
            )
            wr_grouped[g, h] = gr

        def quantise_wr(g, h):
            wr_codes[g, h] = keep.tile([P, HALF], U32, name="wr_codes%d%d" % (g, h), align_bytes=64)
            wr_scales[g, h] = keep.tile([P, HALF], U8, name="wr_scales%d%d" % (g, h), align_bytes=64)
            nc.vector.quantize_mx(out=wr_codes[g, h][:].bitcast(FP8X4), scales=wr_scales[g, h][:], in_=wr_grouped[g, h][:])

        def multiply(i, n0, width):
            op = UNITS[i][0]
            h, m0 = n0 // HALF, n0 % HALF
            acc = acc_psum.tile([P, HALF], F32, name="acc")
            accs[i, n0] = acc
            for g in range(PASSES):
                if op == "k":
                    rhs = wk_w[g][:, 2 * n0 : 2 * (n0 + width)].bitcast(FP4X4)
                    rhs_scale = wk_s[:, g, n0 : n0 + width]
                else:
                    rhs = wr_codes[g, h][:, m0 : m0 + width].bitcast(FP8X4)
                    rhs_scale = wr_scales[g, h][:, m0 : m0 + width]
                nc.tensor.matmul_mx(
                    acc[:, 0:width],
                    lhsT=codes[i][:, P * g : P * (g + 1)].bitcast(FP8X4),
                    lhsT_scale=scales[i][:, P * g : P * (g + 1)],
                    rhs=rhs,
                    rhs_scale=rhs_scale,
                    start=(g == 0),
                    stop=(g == PASSES - 1),
                )

        def empty(i, n0, width):
            op, c = UNITS[i]
            if op == "k":
                if n0 == 0:
                    hidden[c] = keep.tile([P, N], F32, name="hidden%d" % c)
                nc.scalar.activation(hidden[c][:, n0 : n0 + width], accs[i, n0][:, 0:width], ACT.Relu)
            else:
                gates[c, n0] = work.tile([P, HALF], F32, name="gate")
                nc.scalar.activation(gates[c, n0][:, 0:width], accs[i, n0][:, 0:width], ACT.Sigmoid)

        def square(c):
            nc.scalar.activation(hidden[c][:], hidden[c][:], ACT.Square)

        def finish(c, n0, width):
            cols = slice(n0, n0 + width)
            result = work.tile([P, HALF], F32, name="result")
            nc.vector.tensor_tensor(out=result[:, 0:width], in0=gates[c, n0][:, 0:width], in1=hidden[c][:, cols], op=ALU.mult)
            nc.sync.dma_start(out=out_rows[:, c, cols], in_=result[:, 0:width])

        n = len(UNITS)
        for s in range(n + 2):
            if s < n:
                start_wide(s)
                widen_on_vector(s)
            if 1 <= s <= n:
                turn(s - 1)
                collect(s - 1)
            if 0 <= s - SQUARE_STEP < TILES:
                square(s - SQUARE_STEP)
            if s < n:
                widen_on_scalar(s)
            chunk = s - FIRST_CHUNK_STEP
            if 0 <= chunk < len(CHUNKS):
                interleave_wr(*CHUNKS[chunk])
            if 1 <= s <= n:
                quantise(s - 1)
            if s >= 2:
                for n0, width in pieces(s - 2):
                    multiply(s - 2, n0, width)
                    empty(s - 2, n0, width)
                if UNITS[s - 2][0] == "r":
                    for n0, width in pieces(s - 2):
                        finish(UNITS[s - 2][1], n0, width)
            if 0 <= chunk < len(CHUNKS):
                quantise_wr(*CHUNKS[chunk])
